import numpy as np
import ml_dtypes


def mxq(x, axis, fmt="e4m3"):
    dtype, down = {"e4m3": (ml_dtypes.float8_e4m3fn, 7), "e5m2": (ml_dtypes.float8_e5m2, 14)}[fmt]
    v = np.moveaxis(np.asarray(x, np.float32).astype(ml_dtypes.bfloat16).astype(np.float64), axis, -1)
    blocks = v.reshape(v.shape[:-1] + (-1, 32))
    amax = np.abs(blocks).max(-1, keepdims=True)
    byte = np.maximum(np.where(amax > 0, np.frexp(amax)[1] - 1 + 127, 0) - down, 1)
    scale = np.exp2(byte - 127.0)
    codes = (blocks / scale).astype(np.float32).astype(dtype).astype(np.float64)
    return np.moveaxis((codes * scale).reshape(v.shape), -1, axis)


WIDE = False


def mx_kscale(k):
    if not WIDE:
        return np.ones(k)
    levels = np.array([10, -10, 5, -5, 0])
    if k % 512:
        return np.exp2(np.random.permutation(np.resize(levels, k // 32))).repeat(32)
    a = np.empty((k // 512, 16))
    for p in range(k // 512):
        a[p, :8] = np.random.permutation(np.resize(levels, 8))
        for g in range(8):
            far = levels[np.abs(levels - a[p, g]) >= 10]
            a[p, g + 8] = far[np.random.randint(len(far))]
    return np.exp2(a.ravel()).repeat(32)


def f64(x):
    return np.asarray(x).astype(np.float64)


def striped(idx):
    return np.tile(idx.reshape(-1, 16).T, (8, 1)).astype(np.uint16)


def unstriped(offs):
    return offs[:16].T.reshape(-1).astype(np.int64)


def striped8(idx):
    return np.concatenate([x.reshape(-1, 16).T for x in idx]).astype(np.uint16)


def runs(offs, k):
    lists = np.stack([offs[16 * r : 16 * r + 16].T.reshape(-1) for r in range(8)]).astype(np.int64)
    return lists[np.arange(k) % 512 // 64]


def pack_weight(w):
    k, n = w.shape
    w = f64(np.asarray(w, np.float32).astype(ml_dtypes.bfloat16)).reshape(k // 32, 32, n)
    amax = np.abs(w).max(1)
    byte = np.clip(np.where(amax > 0, np.frexp(amax)[1] - 1 + 127 - 7, 1), 1, 254)
    scaled = (w * np.exp2(127.0 - byte)[:, None, :]).reshape(k, n).astype(np.float32)
    words = np.ascontiguousarray(scaled.reshape(k // 512, 128, 4, n).transpose(0, 1, 3, 2)).astype(ml_dtypes.float8_e4m3fn).view(np.uint8)
    return words, np.ascontiguousarray(byte.astype(np.uint8).reshape(k // 512, 16, n))


def unpack_weight(words, scales):
    g, p, n, _ = words.shape
    vals = np.ascontiguousarray(words).view(ml_dtypes.float8_e4m3fn).astype(np.float64) * np.repeat(np.exp2(scales.astype(np.float64) - 127.0), 8, axis=1)[..., None]
    return vals.transpose(0, 1, 3, 2).reshape(g * 512, n)


def relu(v):
    return np.maximum(v, 0.0)


K, T, S, N, H, U = 512, 2048, 256, 512, 512, 1024


def setup_inputs():
    n = np.random.standard_normal
    s = mx_kscale(K)[:, None]
    u = mx_kscale(H)
    packed_xT = pack_weight(n((K, T)) * s)
    return {
        "x_words": packed_xT[0],
        "x_scales": packed_xT[1],
        "w1": (n((K, H)) / np.sqrt(2 * K) / s).astype(np.float32),
        "w2": (n((K, H)) / np.sqrt(2 * K) / s).astype(np.float32),
        "gn": (np.random.uniform(0.5, 1.5, (H, 1)) * u[:, None]).astype(np.float32),
        "w3": (n((H, N)) / np.sqrt(H) / u[:, None]).astype(np.float32),
        "offs": striped8(np.random.randint(0, T, (8, S))),
        "hz": striped8(np.random.randint(0, T, (8, S))),
        "n1": striped(np.random.permutation(S)),
        "n2": striped(np.random.permutation(S)),
        "n3": striped(np.random.permutation(U)[:S]),
        "n4": striped(np.random.permutation(S)),
    }


def reference(x_words, x_scales, w1, w2, gn, w3, offs, hz, n1, n2, n3, n4):
    xq = unpack_weight(x_words, x_scales)[np.arange(K)[:, None], runs(offs, K)]
    x_hz = unpack_weight(x_words, x_scales)[np.arange(K)[:, None], runs(hz, K)]
    y = mxq(f64(w1), 0, "e4m3").T @ xq + mxq(f64(w2), 0, "e4m3").T @ x_hz
    ds = np.zeros((H, S))
    ds[:, unstriped(n1)] = y
    z = f64(gn) * (np.maximum(y, ds[:, unstriped(n2)]))
    h = mxq(f64(w3), 0, "e4m3").T @ mxq(z, 0, "e4m3")
    nw = h - (relu(h[:, unstriped(n4)]))
    out = np.zeros((N, U))
    out[:, unstriped(n3)] = nw
    return out

@@ -1,0 +1,182 @@
+from contextlib import ExitStack
+
+import concourse.mybir as mybir
+
+K, T, S, N, H, U = 512, 2048, 256, 512, 512, 1024
+FLOPS = 2 * (2 * K * H * S) + 2 * H * N * S
+
+F32 = mybir.dt.float32
+BF16 = mybir.dt.bfloat16
+I32 = mybir.dt.int32
+U32 = mybir.dt.uint32
+U16 = mybir.dt.uint16
+U8 = mybir.dt.uint8
+FP8X4 = mybir.dt.float8_e4m3fn_x4
+COPY = mybir.ActivationFunctionType.Copy
+ALU = mybir.AluOpType
+
+P = 128
+PACK = 4
+WIDE = 384
+CHUNK = 64
+
+
+def tile_picked_dhlrelaypagez_none_p_kernel(
+    tc, x_words, x_scales, w1, w2, gn, w3, offs, hz, n1, n2, n3, n4, out
+):
+    nc = tc.nc
+    with ExitStack() as ctx:
+        lists = ctx.enter_context(tc.tile_pool(name="lists", bufs=1))
+        keep = ctx.enter_context(tc.tile_pool(name="keep", bufs=1))
+        raws = ctx.enter_context(tc.tile_pool(name="raws", bufs=1))
+        psum = ctx.enter_context(tc.psum_pool(name="psum", bufs=1))
+
+        def load_list(ap, name):
+            tile = lists.tile([P, S // 16], U16, name=name)
+            nc.sync.dma_start(tile[:], ap)
+            return tile
+
+        def load_weight(w, tag):
+            raw = raws.tile([P, PACK, H], F32, name=tag)
+            nc.sync.dma_start(raw[:], w.rearrange("(p j) c -> p j c", j=PACK))
+            return raw
+
+        byte_table = keep.tile([P, T], U8, name="byte_table")
+        nc.vector.memset(byte_table[:].bitcast(I32), 0)
+        for e in range(2):
+            nc.sync.dma_start(byte_table[e:P:16, :].bitcast(I32), x_scales[0][e:16:2, :].bitcast(I32))
+        w1_raw = load_weight(w1, "raw_a")
+        offs_t = load_list(offs, "offs_t")
+        hz_t = load_list(hz, "hz_t")
+        n1_t = load_list(n1, "n1_t")
+        n2_t = load_list(n2, "n2_t")
+        word_table = keep.tile([P, T], U32, name="word_table")
+        nc.sync.dma_start(word_table[:].bitcast(I32), x_words[0].rearrange("p c r -> p (c r)").bitcast(I32))
+        w2_raw = load_weight(w2, "raw_b")
+        n4_t = load_list(n4, "n4_t")
+        n3_t = load_list(n3, "n3_t")
+        gain = keep.tile([P, PACK], F32, name="gain")
+        nc.sync.dma_start(gain[:], gn.rearrange("(p t) o -> p (t o)", t=PACK))
+
+        picked_bytes = keep.tile([P, 2 * S], U8, name="picked_bytes")
+        x_plane = keep.tile([P, 2 * S], U8, name="x_plane", align_bytes=64)
+        for a, lst in enumerate((offs_t, hz_t)):
+            nc.vector.tensor_copy(picked_bytes[:, a * S : (a + 1) * S], byte_table[:].indirect(lst[:]))
+        nc.vector.tensor_copy(x_plane[:].bitcast(I32), picked_bytes[:].bitcast(I32))
+        for e in range(2):
+            nc.scalar.dma_start(x_plane[2 + e : P : 32, :].bitcast(I32), picked_bytes[16 + e : P : 32, :].bitcast(I32))
+
+        pages = [keep.tile([P, U], F32, name=f"page{t}") for t in range(PACK)]
+        for page in pages:
+            nc.vector.memset(page[:], 0.0)
+
+        w1_bf = keep.tile([P, PACK * H], BF16, name="w1_bf", align_bytes=64)
+        for c in range(PACK):
+            ms = slice(c * P // PACK, (c + 1) * P // PACK)
+            nc.scalar.activation(
+                w1_bf[:].rearrange("p (t m j) -> p m j t", t=PACK, j=PACK)[:, ms],
+                w1_raw[:].rearrange("p j (m t) -> p m j t", t=PACK)[:, ms],
+                COPY,
+            )
+        w1_codes = keep.tile([P, H], U32, name="w1_codes", align_bytes=64)
+        w1_plane = keep.tile([P, H], U8, name="w1_plane", align_bytes=64)
+        nc.vector.quantize_mx(out=w1_codes[:].bitcast(FP8X4), scales=w1_plane[:], in_=w1_bf[:])
+
+        x_codes = []
+        for a, lst in enumerate((offs_t, hz_t)):
+            codes = keep.tile([P, S], U32, name=f"x_codes{a}", align_bytes=64)
+            nc.vector.tensor_copy(codes[:], word_table[:].indirect(lst[:]))
+            x_codes.append(codes)
+
+        y_banks = [psum.tile([P, S], F32, name=f"y{t}") for t in range(PACK)]
+
+        ds = [keep.tile([P, WIDE], F32, name=f"ds{t}") for t in range(PACK)]
+        fetched = keep.tile([P, PACK, S], F32, name="fetched")
+
+        def fetch(t, cols):
+            entries = slice(cols.start // 16, cols.stop // 16)
+            nc.scalar.activation(fetched[:, t, cols], ds[t][:].indirect(n2_t[:, entries]), COPY)
+
+        for t in range(PACK):
+            w2_bf = keep.tile([P, P * PACK], BF16, name=f"w2_bf{t}", tag=f"relay{t % 3}", align_bytes=64)
+            dealt = w2_raw[:].rearrange("p j (m t) -> p t m j", t=PACK)[:, t]
+            if t == 1:
+                nc.scalar.activation(w2_bf[:].rearrange("p (m j) -> p m j", j=PACK), dealt, COPY)
+            else:
+                nc.vector.tensor_copy(w2_bf[:].rearrange("p (m j) -> p m j", j=PACK), dealt)
+            w2_codes = keep.tile([P, P], U32, name=f"w2_codes{t}", tag=f"codes{t}", align_bytes=64)
+            w2_plane = keep.tile([P, P], U8, name=f"w2_plane{t}", tag=f"plane{t}", align_bytes=64)
+            nc.vector.quantize_mx(out=w2_codes[:].bitcast(FP8X4), scales=w2_plane[:], in_=w2_bf[:])
+            cols = slice(t * P, (t + 1) * P)
+            nc.tensor.matmul_mx(
+                out=y_banks[t][:], lhsT=w1_codes[:, cols].bitcast(FP8X4), lhsT_scale=w1_plane[:, cols],
+                rhs=x_codes[0][:].bitcast(FP8X4), rhs_scale=x_plane[:, 0:S], start=True, stop=False,
+            )
+            nc.tensor.matmul_mx(
+                out=y_banks[t][:], lhsT=w2_codes[:].bitcast(FP8X4), lhsT_scale=w2_plane[:],
+                rhs=x_codes[1][:].bitcast(FP8X4), rhs_scale=x_plane[:, S : 2 * S], start=False, stop=True,
+            )
+            y_sb = keep.tile([P, S], F32, name=f"y_sb{t}", tag=f"relay{t % 3}", align_bytes=64)
+            nc.vector.tensor_copy(y_sb[:], y_banks[t][:])
+            nc.scalar.activation(ds[t][:].indirect(n1_t[:]), y_sb[:], COPY)
+            if t < PACK - 1:
+                fetch(t, slice(0, S))
+
+        w3_raw = load_weight(w3, "raw_a")
+        w3_codes, w3_planes = [], []
+        w3_all = keep.tile([P, PACK, P * PACK], BF16, name="w3_all", tag=f"plane{PACK - 1}", align_bytes=64)
+        for t in range(PACK):
+            w3_bf = w3_all[:, t, :]
+            nc.vector.tensor_copy(
+                w3_bf.rearrange("p (c i j) -> p c j i", i=4, j=PACK),
+                w3_raw[:, :, t * P : (t + 1) * P].rearrange("p j (c i) -> p c j i", i=4),
+            )
+            codes = keep.tile([P, P], U32, name=f"w3_codes{t}", align_bytes=64)
+            plane = keep.tile([P, P], U8, name=f"w3_plane{t}", align_bytes=64)
+            nc.vector.quantize_mx(out=codes[:].bitcast(FP8X4), scales=plane[:], in_=w3_bf)
+            w3_codes.append(codes)
+            w3_planes.append(plane)
+
+        larger = keep.tile([P, PACK, S], F32, name="larger", tag=f"codes{PACK - 1}", align_bytes=64)
+        z_bf = keep.tile([P, S * PACK], BF16, name="z_bf", align_bytes=64)
+
+        def make_z(t, cols):
+            nc.vector.tensor_tensor(larger[:, t, cols], y_banks[t][:, cols], fetched[:, t, cols], ALU.max)
+            nc.vector.tensor_scalar_mul(
+                z_bf[:].rearrange("p (c t) -> p t c", t=PACK)[:, t, cols], larger[:, t, cols], gain[:, t : t + 1]
+            )
+
+        for t in range(PACK - 1):
+            make_z(t, slice(0, S))
+        h_banks = [psum.tile([P, S], F32, name=f"h{t}") for t in range(PACK)]
+        z_codes = keep.tile([P, S], U32, name="z_codes", align_bytes=64)
+        z_plane = keep.tile([P, S], U8, name="z_plane", align_bytes=64)
+
+        def second_product(t, cols):
+            nc.tensor.matmul_mx(
+                out=h_banks[t][:, cols], lhsT=w3_codes[t][:].bitcast(FP8X4), lhsT_scale=w3_planes[t][:],
+                rhs=z_codes[:, cols].bitcast(FP8X4), rhs_scale=z_plane[:, cols], start=True, stop=True,
+            )
+
+        for q in range(S // CHUNK):
+            cols = slice(q * CHUNK, (q + 1) * CHUNK)
+            fetch(PACK - 1, cols)
+            make_z(PACK - 1, cols)
+            nc.vector.quantize_mx(
+                out=z_codes[:, cols].bitcast(FP8X4), scales=z_plane[:, cols],
+                in_=z_bf[:, cols.start * PACK : cols.stop * PACK],
+            )
+            second_product(0, cols)
+        for t in range(1, PACK):
+            second_product(t, slice(0, S))
+
+        pulled = keep.tile([P, PACK, S], F32, name="pulled")
+        for t in range(PACK):
+            positive = keep.tile([P, WIDE], F32, name=f"positive{t}")
+            nc.vector.tensor_scalar_max(positive[:, 0:S], h_banks[t][:], 0.0)
+            nc.scalar.activation(pulled[:, t, :], positive[:].indirect(n4_t[:]), COPY)
+        for t in range(PACK):
+            nw = keep.tile([P, S], F32, name=f"nw{t}")
+            nc.vector.tensor_tensor(nw[:], h_banks[t][:], pulled[:, t, :], ALU.subtract)
+            nc.scalar.activation(pages[t][:].indirect(n3_t[:]), nw[:], COPY)
+            nc.sync.dma_start(out[t * P : (t + 1) * P, :], pages[t][:])

@@ -13,12 +13,14 @@ U16 = mybir.dt.uint16
 U8 = mybir.dt.uint8
 FP8X4 = mybir.dt.float8_e4m3fn_x4
 COPY = mybir.ActivationFunctionType.Copy
+RELU = mybir.ActivationFunctionType.Relu
 ALU = mybir.AluOpType
 
 P = 128
 PACK = 4
 WIDE = 384
 CHUNK = 64
+HALF = H // 2
 
 
 def tile_picked_dhlrelaypagez_none_p_kernel(
@@ -28,7 +30,6 @@ def tile_picked_dhlrelaypagez_none_p_kernel(
     with ExitStack() as ctx:
         lists = ctx.enter_context(tc.tile_pool(name="lists", bufs=1))
         keep = ctx.enter_context(tc.tile_pool(name="keep", bufs=1))
-        raws = ctx.enter_context(tc.tile_pool(name="raws", bufs=1))
         psum = ctx.enter_context(tc.psum_pool(name="psum", bufs=1))
 
         def load_list(ap, name):
@@ -36,51 +37,67 @@ def tile_picked_dhlrelaypagez_none_p_kernel(
             nc.sync.dma_start(tile[:], ap)
             return tile
 
-        def load_weight(w, tag):
-            raw = raws.tile([P, PACK, H], F32, name=tag)
-            nc.sync.dma_start(raw[:], w.rearrange("(p j) c -> p j c", j=PACK))
+        def load_columns(w, first, width, tag):
+            raw = keep.tile([P, PACK, width], F32, name=f"raw_{tag}", tag=tag, align_bytes=64)
+            nc.sync.dma_start(raw[:], w.rearrange("(p j) c -> p j c", j=PACK)[:, :, first : first + width])
             return raw
 
-        byte_table = keep.tile([P, T], U8, name="byte_table")
+        def round_pair(on_scalar, staged, raw, s0):
+            dst = staged.rearrange("p s m j -> p m j s")
+            src = raw.rearrange("p j (m s) -> p m j s", s=PACK)[:, :, :, s0 : s0 + 2]
+            if on_scalar:
+                nc.scalar.activation(dst, src, COPY)
+            else:
+                nc.vector.tensor_copy(dst, src)
+
+        def quantise(staged, name, codes_tag=None, plane_tag=None):
+            words = staged.shape[1] // PACK
+            codes = keep.tile([P, words], U32, name=f"{name}_codes", tag=codes_tag or f"{name}_codes", align_bytes=64)
+            plane = keep.tile([P, words], U8, name=f"{name}_plane", tag=plane_tag or f"{name}_plane", align_bytes=64)
+            nc.vector.quantize_mx(out=codes[:].bitcast(FP8X4), scales=plane[:], in_=staged)
+            return codes, plane
+
+        def product(bank, weights, first, codes, plane, start, stop):
+            nc.tensor.matmul_mx(
+                out=bank, lhsT=weights[0][:, first : first + P].bitcast(FP8X4),
+                lhsT_scale=weights[1][:, first : first + P],
+                rhs=codes.bitcast(FP8X4), rhs_scale=plane, start=start, stop=stop,
+            )
+
+        byte_table = keep.tile([P, T], U8, name="byte_table", align_bytes=64)
         nc.vector.memset(byte_table[:].bitcast(I32), 0)
         for e in range(2):
             nc.sync.dma_start(byte_table[e:P:16, :].bitcast(I32), x_scales[0][e:16:2, :].bitcast(I32))
-        w1_raw = load_weight(w1, "raw_a")
+        w1_low = load_columns(w1, 0, HALF, "w1_low")
         offs_t = load_list(offs, "offs_t")
         hz_t = load_list(hz, "hz_t")
         n1_t = load_list(n1, "n1_t")
         n2_t = load_list(n2, "n2_t")
         word_table = keep.tile([P, T], U32, name="word_table")
         nc.sync.dma_start(word_table[:].bitcast(I32), x_words[0].rearrange("p c r -> p (c r)").bitcast(I32))
-        w2_raw = load_weight(w2, "raw_b")
+        w2_low = load_columns(w2, 0, HALF, "w2_low")
         n4_t = load_list(n4, "n4_t")
         n3_t = load_list(n3, "n3_t")
-        gain = keep.tile([P, PACK], F32, name="gain")
-        nc.sync.dma_start(gain[:], gn.rearrange("(p t) o -> p (t o)", t=PACK))
 
         picked_bytes = keep.tile([P, 2 * S], U8, name="picked_bytes")
         x_plane = keep.tile([P, 2 * S], U8, name="x_plane", align_bytes=64)
+        nc.vector.memset(x_plane[:].bitcast(I32), 0)
         for a, lst in enumerate((offs_t, hz_t)):
             nc.vector.tensor_copy(picked_bytes[:, a * S : (a + 1) * S], byte_table[:].indirect(lst[:]))
-        nc.vector.tensor_copy(x_plane[:].bitcast(I32), picked_bytes[:].bitcast(I32))
         for e in range(2):
-            nc.scalar.dma_start(x_plane[2 + e : P : 32, :].bitcast(I32), picked_bytes[16 + e : P : 32, :].bitcast(I32))
+            nc.sync.dma_start(x_plane[2 + e : P : 32, :].bitcast(I32), picked_bytes[16 + e : P : 32, :].bitcast(I32))
+        highs = keep.tile([P, 2, PACK, HALF], F32, name="highs", tag="byte_table", align_bytes=64)
+        for u, w in enumerate((w1, w2)):
+            nc.sync.dma_start(highs[:, u], w.rearrange("(p j) c -> p j c", j=PACK)[:, :, HALF:H])
+        w1_high, w2_high = highs[:, 0], highs[:, 1]
+        for q in range(4):
+            rows = slice(32 * q, 32 * q + 2)
+            nc.vector.tensor_copy(x_plane[rows, :].bitcast(I32), picked_bytes[rows, :].bitcast(I32))
 
         pages = [keep.tile([P, U], F32, name=f"page{t}") for t in range(PACK)]
-        for page in pages:
-            nc.vector.memset(page[:], 0.0)
-
-        w1_bf = keep.tile([P, PACK * H], BF16, name="w1_bf", align_bytes=64)
-        for c in range(PACK):
-            ms = slice(c * P // PACK, (c + 1) * P // PACK)
-            nc.scalar.activation(
-                w1_bf[:].rearrange("p (t m j) -> p m j t", t=PACK, j=PACK)[:, ms],
-                w1_raw[:].rearrange("p j (m t) -> p m j t", t=PACK)[:, ms],
-                COPY,
-            )
-        w1_codes = keep.tile([P, H], U32, name="w1_codes", align_bytes=64)
-        w1_plane = keep.tile([P, H], U8, name="w1_plane", align_bytes=64)
-        nc.vector.quantize_mx(out=w1_codes[:].bitcast(FP8X4), scales=w1_plane[:], in_=w1_bf[:])
+        for t in range(2):
+            nc.vector.memset(pages[t][:], 0.0)
+            nc.scalar.activation(pages[2 + t][:], pages[t][:], COPY)
 
         x_codes = []
         for a, lst in enumerate((offs_t, hz_t)):
@@ -88,95 +105,157 @@ def tile_picked_dhlrelaypagez_none_p_kernel(
             nc.vector.tensor_copy(codes[:], word_table[:].indirect(lst[:]))
             x_codes.append(codes)
 
-        y_banks = [psum.tile([P, S], F32, name=f"y{t}") for t in range(PACK)]
+        def stage(name, tag=None):
+            return keep.tile([P, 2, P // 2, PACK], BF16, name=name, tag=tag or name, align_bytes=64)
 
+        def flat(staged):
+            return staged[:].rearrange("p s m j -> p (s m j)")
+
+        def quantise_cd(staged, half, codes, plane):
+            for u in range(2):
+                cols = slice(u * P + half * P // 2, u * P + (half + 1) * P // 2)
+                nc.vector.quantize_mx(
+                    out=codes[:, cols].bitcast(FP8X4), scales=plane[:, cols],
+                    in_=staged[:, u].rearrange("p m j -> p (m j)"),
+                )
+
+        bank_a = psum.tile([P, S], F32, name="bank_a")
+        bank_b = psum.tile([P, S], F32, name="bank_b")
+        bank_cd = psum.tile([P, 2, S], F32, name="bank_cd")
+        y_banks = [bank_a[:], bank_b[:], bank_cd[:, 0], bank_cd[:, 1]]
         ds = [keep.tile([P, WIDE], F32, name=f"ds{t}") for t in range(PACK)]
         fetched = keep.tile([P, PACK, S], F32, name="fetched")
+
+        def first_layer(t, q1, q2, first):
+            product(y_banks[t], q1, first, x_codes[0][:], x_plane[:, 0:S], True, False)
+            product(y_banks[t], q2, first, x_codes[1][:], x_plane[:, S : 2 * S], False, True)
+
+        def send(t, y_sb, cols):
+            entries = slice(cols.start // 16, cols.stop // 16)
+            nc.scalar.activation(ds[t][:].indirect(n1_t[:, entries]), y_sb[:, cols], COPY)
 
         def fetch(t, cols):
             entries = slice(cols.start // 16, cols.stop // 16)
             nc.scalar.activation(fetched[:, t, cols], ds[t][:].indirect(n2_t[:, entries]), COPY)
 
-        for t in range(PACK):
-            w2_bf = keep.tile([P, P * PACK], BF16, name=f"w2_bf{t}", tag=f"relay{t % 3}", align_bytes=64)
-            dealt = w2_raw[:].rearrange("p j (m t) -> p t m j", t=PACK)[:, t]
-            if t == 1:
-                nc.scalar.activation(w2_bf[:].rearrange("p (m j) -> p m j", j=PACK), dealt, COPY)
-            else:
-                nc.vector.tensor_copy(w2_bf[:].rearrange("p (m j) -> p m j", j=PACK), dealt)
-            w2_codes = keep.tile([P, P], U32, name=f"w2_codes{t}", tag=f"codes{t}", align_bytes=64)
-            w2_plane = keep.tile([P, P], U8, name=f"w2_plane{t}", tag=f"plane{t}", align_bytes=64)
-            nc.vector.quantize_mx(out=w2_codes[:].bitcast(FP8X4), scales=w2_plane[:], in_=w2_bf[:])
-            cols = slice(t * P, (t + 1) * P)
-            nc.tensor.matmul_mx(
-                out=y_banks[t][:], lhsT=w1_codes[:, cols].bitcast(FP8X4), lhsT_scale=w1_plane[:, cols],
-                rhs=x_codes[0][:].bitcast(FP8X4), rhs_scale=x_plane[:, 0:S], start=True, stop=False,
-            )
-            nc.tensor.matmul_mx(
-                out=y_banks[t][:], lhsT=w2_codes[:].bitcast(FP8X4), lhsT_scale=w2_plane[:],
-                rhs=x_codes[1][:].bitcast(FP8X4), rhs_scale=x_plane[:, S : 2 * S], start=False, stop=True,
-            )
-            y_sb = keep.tile([P, S], F32, name=f"y_sb{t}", tag=f"relay{t % 3}", align_bytes=64)
-            nc.vector.tensor_copy(y_sb[:], y_banks[t][:])
-            nc.scalar.activation(ds[t][:].indirect(n1_t[:]), y_sb[:], COPY)
-            if t < PACK - 1:
-                fetch(t, slice(0, S))
+        whole = slice(0, S)
+        q1_cd = [keep.tile([P, 2 * P], dtype, name=f"q1_cd{n}", align_bytes=64) for n, dtype in enumerate((U32, U8))]
+        q2_cd = [keep.tile([P, 2 * P], dtype, name=f"q2_cd{n}", align_bytes=64) for n, dtype in enumerate((U32, U8))]
 
-        w3_raw = load_weight(w3, "raw_a")
-        w3_codes, w3_planes = [], []
-        w3_all = keep.tile([P, PACK, P * PACK], BF16, name="w3_all", tag=f"plane{PACK - 1}", align_bytes=64)
-        for t in range(PACK):
-            w3_bf = w3_all[:, t, :]
-            nc.vector.tensor_copy(
-                w3_bf.rearrange("p (c i j) -> p c j i", i=4, j=PACK),
-                w3_raw[:, :, t * P : (t + 1) * P].rearrange("p j (c i) -> p c j i", i=4),
-            )
-            codes = keep.tile([P, P], U32, name=f"w3_codes{t}", align_bytes=64)
-            plane = keep.tile([P, P], U8, name=f"w3_plane{t}", align_bytes=64)
-            nc.vector.quantize_mx(out=codes[:].bitcast(FP8X4), scales=plane[:], in_=w3_bf)
-            w3_codes.append(codes)
-            w3_planes.append(plane)
+        w1_a, w1_cd_low, w2_a, w2_cd_low, w1_b = (stage(n) for n in ("w1_a", "w1_cd_low", "w2_a", "w2_cd_low", "w1_b"))
+        round_pair(True, w1_a[:], w1_low[:], 0)
+        round_pair(True, w1_cd_low[:], w1_low[:], 2)
+        q1_a = quantise(flat(w1_a), "q1_a")
+        quantise_cd(w1_cd_low, 0, *q1_cd)
+        round_pair(False, w2_a[:], w2_low[:], 0)
+        q2_a = quantise(flat(w2_a), "q2_a")
+        round_pair(True, w2_cd_low[:], w2_low[:], 2)
+        round_pair(True, w1_b[:], w1_high, 0)
+        first_layer(0, q1_a, q2_a, 0)
+        y_a = keep.tile([P, S], F32, name="y_a")
+        nc.vector.tensor_copy(y_a[:], y_banks[0])
+        send(0, y_a, whole)
+        fetch(0, whole)
+        quantise_cd(w2_cd_low, 0, *q2_cd)
 
-        larger = keep.tile([P, PACK, S], F32, name="larger", tag=f"codes{PACK - 1}", align_bytes=64)
+        q1_b = quantise(flat(w1_b), "q1_b", codes_tag="q2_a_codes")
+        w2_b = stage("w2_b", tag="q2_a_plane")
+        round_pair(False, w2_b[:], w2_high, 0)
+        q2_b = quantise(flat(w2_b), "q2_b")
+        first_layer(1, q1_b, q2_b, 0)
+        y_b = keep.tile([P, S], F32, name="y_b")
+        nc.vector.tensor_copy(y_b[:], y_banks[1])
+        send(1, y_b, whole)
+        fetch(1, whole)
+
+        gain = keep.tile([P, PACK], F32, name="gain", tag="w2_low", align_bytes=64)
+        nc.sync.dma_start(gain[:], gn.rearrange("(p t) o -> p (t o)", t=PACK))
+        w3_raw = load_columns(w3, 0, N, "w2_a")
+
+        cd_high = keep.tile([P, 2, 2, P // 2, PACK], BF16, name="cd_high", tag="q2_a_plane", align_bytes=64)
+        round_pair(False, cd_high[:, 0], w1_high, 2)
+        round_pair(False, cd_high[:, 1], w2_high, 2)
+        quantise_cd(cd_high[:, 0], 1, *q1_cd)
+        quantise_cd(cd_high[:, 1], 1, *q2_cd)
+        first_layer(2, q1_cd, q2_cd, 0)
+        first_layer(3, q1_cd, q2_cd, P)
+        y_cd = keep.tile([P, 2, S], F32, name="y_cd")
+        nc.vector.tensor_copy(y_cd[:], bank_cd[:])
+        send(2, y_cd[:, 0], whole)
+        send(3, y_cd[:, 1], slice(0, S // 2))
+        fetch(2, whole)
+        send(3, y_cd[:, 1], slice(S // 2, S))
+
         z_bf = keep.tile([P, S * PACK], BF16, name="z_bf", align_bytes=64)
+        z_slots = z_bf[:].rearrange("p (c t) -> p t c", t=PACK)
+        low, high, every = slice(0, P // 2), slice(P // 2, P), slice(0, P)
 
-        def make_z(t, cols):
-            nc.vector.tensor_tensor(larger[:, t, cols], y_banks[t][:, cols], fetched[:, t, cols], ALU.max)
-            nc.vector.tensor_scalar_mul(
-                z_bf[:].rearrange("p (c t) -> p t c", t=PACK)[:, t, cols], larger[:, t, cols], gain[:, t : t + 1]
+        def larger_of(t, cols, larger):
+            nc.vector.tensor_tensor(larger[:, cols], y_banks[t][:, cols], fetched[:, t, cols], ALU.max)
+
+        def put_z(parts, slot, cols, larger):
+            nc.vector.tensor_scalar_mul(z_slots[parts, slot, cols], larger[parts, cols], gain[parts, slot : slot + 1])
+
+        q3 = []
+
+        def quantise_w3(u):
+            staged = keep.tile([P, HALF * PACK], BF16, name=f"w3_bf{u}", align_bytes=64)
+            nc.vector.tensor_copy(
+                staged[:].rearrange("p (c i j) -> p c j i", i=4, j=PACK),
+                w3_raw[:, :, u * HALF : (u + 1) * HALF].rearrange("p j (c i) -> p c j i", i=4),
             )
+            q3.append(quantise(staged[:], f"q3_{u}"))
 
-        for t in range(PACK - 1):
-            make_z(t, slice(0, S))
+        larger_a = keep.tile([P, S], F32, name="larger_a", tag="q2_a_plane", align_bytes=64)
+        moved = keep.tile([P, S], F32, name="moved")
+        larger_of(0, whole, larger_a)
+        nc.sync.dma_start(moved[low, :], larger_a[high, :])
+        quantise_w3(0)
+        larger_b = keep.tile([P, S], F32, name="larger_b", tag="w3_bf0", align_bytes=64)
+        larger_of(1, whole, larger_b)
+        nc.sync.dma_start(larger_a[high, :], larger_b[low, :])
+        put_z(high, 1, whole, larger_b)
+        quantise_w3(1)
+        put_z(low, 1, whole, moved)
+        larger_c = keep.tile([P, S], F32, name="larger_c", tag="w3_bf1", align_bytes=64)
+        put_z(every, 0, whole, larger_a)
+        larger_of(2, whole, larger_c)
+        put_z(every, 2, whole, larger_c)
+        larger_d = keep.tile([P, S], F32, name="larger_d", tag="q2_a_plane", align_bytes=64)
+
         h_banks = [psum.tile([P, S], F32, name=f"h{t}") for t in range(PACK)]
+        h_last = psum.tile([P, CHUNK], F32, name="h_last")
         z_codes = keep.tile([P, S], U32, name="z_codes", align_bytes=64)
         z_plane = keep.tile([P, S], U8, name="z_plane", align_bytes=64)
-
-        def second_product(t, cols):
-            nc.tensor.matmul_mx(
-                out=h_banks[t][:, cols], lhsT=w3_codes[t][:].bitcast(FP8X4), lhsT_scale=w3_planes[t][:],
-                rhs=z_codes[:, cols].bitcast(FP8X4), rhs_scale=z_plane[:, cols], start=True, stop=True,
-            )
-
-        for q in range(S // CHUNK):
-            cols = slice(q * CHUNK, (q + 1) * CHUNK)
+        for cols in (slice(0, S - 2 * CHUNK), slice(S - 2 * CHUNK, S - CHUNK), slice(S - CHUNK, S)):
             fetch(PACK - 1, cols)
-            make_z(PACK - 1, cols)
+            larger_of(PACK - 1, cols, larger_d)
+            put_z(every, PACK - 1, cols, larger_d)
             nc.vector.quantize_mx(
                 out=z_codes[:, cols].bitcast(FP8X4), scales=z_plane[:, cols],
                 in_=z_bf[:, cols.start * PACK : cols.stop * PACK],
             )
-            second_product(0, cols)
+            bank = h_banks[0][:, cols] if cols.stop < S else h_last[:]
+            product(bank, q3[0], 0, z_codes[:, cols], z_plane[:, cols], True, True)
         for t in range(1, PACK):
-            second_product(t, slice(0, S))
+            product(h_banks[t][:], q3[t // 2], t % 2 * P, z_codes[:], z_plane[:], True, True)
 
+        early, late = slice(0, S - CHUNK), slice(S - CHUNK, S)
         pulled = keep.tile([P, PACK, S], F32, name="pulled")
         for t in range(PACK):
             positive = keep.tile([P, WIDE], F32, name=f"positive{t}")
-            nc.vector.tensor_scalar_max(positive[:, 0:S], h_banks[t][:], 0.0)
+            if t == 0:
+                nc.scalar.activation(positive[:, early], h_banks[0][:, early], RELU)
+                nc.scalar.activation(positive[:, late], h_last[:], RELU)
+            else:
+                nc.vector.tensor_scalar_max(positive[:, 0:S], h_banks[t][:], 0.0)
             nc.scalar.activation(pulled[:, t, :], positive[:].indirect(n4_t[:]), COPY)
         for t in range(PACK):
             nw = keep.tile([P, S], F32, name=f"nw{t}")
-            nc.vector.tensor_tensor(nw[:], h_banks[t][:], pulled[:, t, :], ALU.subtract)
+            if t == 0:
+                nc.vector.tensor_tensor(nw[:, early], h_banks[0][:, early], pulled[:, 0, early], ALU.subtract)
+                nc.vector.tensor_tensor(nw[:, late], h_last[:], pulled[:, 0, late], ALU.subtract)
+            else:
+                nc.vector.tensor_tensor(nw[:], h_banks[t][:], pulled[:, t, :], ALU.subtract)
             nc.scalar.activation(pages[t][:].indirect(n3_t[:]), nw[:], COPY)
             nc.sync.dma_start(out[t * P : (t + 1) * P, :], pages[t][:])

from contextlib import ExitStack

import concourse.mybir as mybir

K, T, S, N, H, U = 512, 2048, 256, 512, 512, 1024
FLOPS = 2 * (2 * K * H * S) + 2 * H * N * S

F32 = mybir.dt.float32
BF16 = mybir.dt.bfloat16
I32 = mybir.dt.int32
U32 = mybir.dt.uint32
U16 = mybir.dt.uint16
U8 = mybir.dt.uint8
FP8X4 = mybir.dt.float8_e4m3fn_x4
COPY = mybir.ActivationFunctionType.Copy
RELU = mybir.ActivationFunctionType.Relu
ALU = mybir.AluOpType

P = 128
PACK = 4
WIDE = 384
CHUNK = 64
HALF = H // 2


def tile_picked_dhlrelaypagez_none_p_kernel(
    tc, x_words, x_scales, w1, w2, gn, w3, offs, hz, n1, n2, n3, n4, out
):
    nc = tc.nc
    with ExitStack() as ctx:
        lists = ctx.enter_context(tc.tile_pool(name="lists", bufs=1))
        keep = ctx.enter_context(tc.tile_pool(name="keep", bufs=1))
        psum = ctx.enter_context(tc.psum_pool(name="psum", bufs=1))

        def load_list(ap, name):
            tile = lists.tile([P, S // 16], U16, name=name)
            nc.sync.dma_start(tile[:], ap)
            return tile

        def load_columns(w, first, width, tag):
            raw = keep.tile([P, PACK, width], F32, name=f"raw_{tag}", tag=tag, align_bytes=64)
            nc.sync.dma_start(raw[:], w.rearrange("(p j) c -> p j c", j=PACK)[:, :, first : first + width])
            return raw

        def round_pair(on_scalar, staged, raw, s0):
            dst = staged.rearrange("p s m j -> p m j s")
            src = raw.rearrange("p j (m s) -> p m j s", s=PACK)[:, :, :, s0 : s0 + 2]
            if on_scalar:
                nc.scalar.activation(dst, src, COPY)
            else:
                nc.vector.tensor_copy(dst, src)

        def quantise(staged, name, codes_tag=None, plane_tag=None):
            words = staged.shape[1] // PACK
            codes = keep.tile([P, words], U32, name=f"{name}_codes", tag=codes_tag or f"{name}_codes", align_bytes=64)
            plane = keep.tile([P, words], U8, name=f"{name}_plane", tag=plane_tag or f"{name}_plane", align_bytes=64)
            nc.vector.quantize_mx(out=codes[:].bitcast(FP8X4), scales=plane[:], in_=staged)
            return codes, plane

        def product(bank, weights, first, codes, plane, start, stop):
            nc.tensor.matmul_mx(
                out=bank, lhsT=weights[0][:, first : first + P].bitcast(FP8X4),
                lhsT_scale=weights[1][:, first : first + P],
                rhs=codes.bitcast(FP8X4), rhs_scale=plane, start=start, stop=stop,
            )

        byte_table = keep.tile([P, T], U8, name="byte_table", align_bytes=64)
        nc.vector.memset(byte_table[:].bitcast(I32), 0)
        for e in range(2):
            nc.sync.dma_start(byte_table[e:P:16, :].bitcast(I32), x_scales[0][e:16:2, :].bitcast(I32))
        w1_low = load_columns(w1, 0, HALF, "w1_low")
        offs_t = load_list(offs, "offs_t")
        hz_t = load_list(hz, "hz_t")
        n1_t = load_list(n1, "n1_t")
        n2_t = load_list(n2, "n2_t")
        word_table = keep.tile([P, T], U32, name="word_table")
        nc.sync.dma_start(word_table[:].bitcast(I32), x_words[0].rearrange("p c r -> p (c r)").bitcast(I32))
        w2_low = load_columns(w2, 0, HALF, "w2_low")
        n4_t = load_list(n4, "n4_t")
        n3_t = load_list(n3, "n3_t")

        picked_bytes = keep.tile([P, 2 * S], U8, name="picked_bytes")
        x_plane = keep.tile([P, 2 * S], U8, name="x_plane", align_bytes=64)
        nc.vector.memset(x_plane[:].bitcast(I32), 0)
        for a, lst in enumerate((offs_t, hz_t)):
            nc.vector.tensor_copy(picked_bytes[:, a * S : (a + 1) * S], byte_table[:].indirect(lst[:]))
        for e in range(2):
            nc.sync.dma_start(x_plane[2 + e : P : 32, :].bitcast(I32), picked_bytes[16 + e : P : 32, :].bitcast(I32))
        highs = keep.tile([P, 2, PACK, HALF], F32, name="highs", tag="byte_table", align_bytes=64)
        for u, w in enumerate((w1, w2)):
            nc.sync.dma_start(highs[:, u], w.rearrange("(p j) c -> p j c", j=PACK)[:, :, HALF:H])
        w1_high, w2_high = highs[:, 0], highs[:, 1]
        for q in range(4):
            rows = slice(32 * q, 32 * q + 2)
            nc.vector.tensor_copy(x_plane[rows, :].bitcast(I32), picked_bytes[rows, :].bitcast(I32))

        pages = [keep.tile([P, U], F32, name=f"page{t}") for t in range(PACK)]
        for t in range(2):
            nc.vector.memset(pages[t][:], 0.0)
            nc.scalar.activation(pages[2 + t][:], pages[t][:], COPY)

        x_codes = []
        for a, lst in enumerate((offs_t, hz_t)):
            codes = keep.tile([P, S], U32, name=f"x_codes{a}", align_bytes=64)
            nc.vector.tensor_copy(codes[:], word_table[:].indirect(lst[:]))
            x_codes.append(codes)

        def stage(name, tag=None):
            return keep.tile([P, 2, P // 2, PACK], BF16, name=name, tag=tag or name, align_bytes=64)

        def flat(staged):
            return staged[:].rearrange("p s m j -> p (s m j)")

        def quantise_cd(staged, half, codes, plane):
            for u in range(2):
                cols = slice(u * P + half * P // 2, u * P + (half + 1) * P // 2)
                nc.vector.quantize_mx(
                    out=codes[:, cols].bitcast(FP8X4), scales=plane[:, cols],
                    in_=staged[:, u].rearrange("p m j -> p (m j)"),
                )

        bank_a = psum.tile([P, S], F32, name="bank_a")
        bank_b = psum.tile([P, S], F32, name="bank_b")
        bank_cd = psum.tile([P, 2, S], F32, name="bank_cd")
        y_banks = [bank_a[:], bank_b[:], bank_cd[:, 0], bank_cd[:, 1]]
        ds = [keep.tile([P, WIDE], F32, name=f"ds{t}") for t in range(PACK)]
        fetched = keep.tile([P, PACK, S], F32, name="fetched")

        def first_layer(t, q1, q2, first):
            product(y_banks[t], q1, first, x_codes[0][:], x_plane[:, 0:S], True, False)
            product(y_banks[t], q2, first, x_codes[1][:], x_plane[:, S : 2 * S], False, True)

        def send(t, y_sb, cols):
            entries = slice(cols.start // 16, cols.stop // 16)
            nc.scalar.activation(ds[t][:].indirect(n1_t[:, entries]), y_sb[:, cols], COPY)

        def fetch(t, cols):
            entries = slice(cols.start // 16, cols.stop // 16)
            nc.scalar.activation(fetched[:, t, cols], ds[t][:].indirect(n2_t[:, entries]), COPY)

        whole = slice(0, S)
        q1_cd = [keep.tile([P, 2 * P], dtype, name=f"q1_cd{n}", align_bytes=64) for n, dtype in enumerate((U32, U8))]
        q2_cd = [keep.tile([P, 2 * P], dtype, name=f"q2_cd{n}", align_bytes=64) for n, dtype in enumerate((U32, U8))]

        w1_a, w1_cd_low, w2_a, w2_cd_low, w1_b = (stage(n) for n in ("w1_a", "w1_cd_low", "w2_a", "w2_cd_low", "w1_b"))
        round_pair(True, w1_a[:], w1_low[:], 0)
        round_pair(True, w1_cd_low[:], w1_low[:], 2)
        q1_a = quantise(flat(w1_a), "q1_a")
        quantise_cd(w1_cd_low, 0, *q1_cd)
        round_pair(False, w2_a[:], w2_low[:], 0)
        q2_a = quantise(flat(w2_a), "q2_a")
        round_pair(True, w2_cd_low[:], w2_low[:], 2)
        round_pair(True, w1_b[:], w1_high, 0)
        first_layer(0, q1_a, q2_a, 0)
        y_a = keep.tile([P, S], F32, name="y_a")
        nc.vector.tensor_copy(y_a[:], y_banks[0])
        send(0, y_a, whole)
        fetch(0, whole)
        quantise_cd(w2_cd_low, 0, *q2_cd)

        q1_b = quantise(flat(w1_b), "q1_b", codes_tag="q2_a_codes")
        w2_b = stage("w2_b", tag="q2_a_plane")
        round_pair(False, w2_b[:], w2_high, 0)
        q2_b = quantise(flat(w2_b), "q2_b")
        first_layer(1, q1_b, q2_b, 0)
        y_b = keep.tile([P, S], F32, name="y_b")
        nc.vector.tensor_copy(y_b[:], y_banks[1])
        send(1, y_b, whole)
        fetch(1, whole)

        gain = keep.tile([P, PACK], F32, name="gain", tag="w2_low", align_bytes=64)
        nc.sync.dma_start(gain[:], gn.rearrange("(p t) o -> p (t o)", t=PACK))
        w3_raw = load_columns(w3, 0, N, "w2_a")

        cd_high = keep.tile([P, 2, 2, P // 2, PACK], BF16, name="cd_high", tag="q2_a_plane", align_bytes=64)
        round_pair(False, cd_high[:, 0], w1_high, 2)
        round_pair(False, cd_high[:, 1], w2_high, 2)
        quantise_cd(cd_high[:, 0], 1, *q1_cd)
        quantise_cd(cd_high[:, 1], 1, *q2_cd)
        first_layer(2, q1_cd, q2_cd, 0)
        first_layer(3, q1_cd, q2_cd, P)
        y_cd = keep.tile([P, 2, S], F32, name="y_cd")
        nc.vector.tensor_copy(y_cd[:], bank_cd[:])
        send(2, y_cd[:, 0], whole)
        send(3, y_cd[:, 1], slice(0, S // 2))
        fetch(2, whole)
        send(3, y_cd[:, 1], slice(S // 2, S))

        z_bf = keep.tile([P, S * PACK], BF16, name="z_bf", align_bytes=64)
        z_slots = z_bf[:].rearrange("p (c t) -> p t c", t=PACK)
        low, high, every = slice(0, P // 2), slice(P // 2, P), slice(0, P)

        def larger_of(t, cols, larger):
            nc.vector.tensor_tensor(larger[:, cols], y_banks[t][:, cols], fetched[:, t, cols], ALU.max)

        def put_z(parts, slot, cols, larger):
            nc.vector.tensor_scalar_mul(z_slots[parts, slot, cols], larger[parts, cols], gain[parts, slot : slot + 1])

        q3 = []

        def quantise_w3(u):
            staged = keep.tile([P, HALF * PACK], BF16, name=f"w3_bf{u}", align_bytes=64)
            nc.vector.tensor_copy(
                staged[:].rearrange("p (c i j) -> p c j i", i=4, j=PACK),
                w3_raw[:, :, u * HALF : (u + 1) * HALF].rearrange("p j (c i) -> p c j i", i=4),
            )
            q3.append(quantise(staged[:], f"q3_{u}"))

        larger_a = keep.tile([P, S], F32, name="larger_a", tag="q2_a_plane", align_bytes=64)
        moved = keep.tile([P, S], F32, name="moved")
        larger_of(0, whole, larger_a)
        nc.sync.dma_start(moved[low, :], larger_a[high, :])
        quantise_w3(0)
        larger_b = keep.tile([P, S], F32, name="larger_b", tag="w3_bf0", align_bytes=64)
        larger_of(1, whole, larger_b)
        nc.sync.dma_start(larger_a[high, :], larger_b[low, :])
        put_z(high, 1, whole, larger_b)
        quantise_w3(1)
        put_z(low, 1, whole, moved)
        larger_c = keep.tile([P, S], F32, name="larger_c", tag="w3_bf1", align_bytes=64)
        put_z(every, 0, whole, larger_a)
        larger_of(2, whole, larger_c)
        put_z(every, 2, whole, larger_c)
        larger_d = keep.tile([P, S], F32, name="larger_d", tag="q2_a_plane", align_bytes=64)

        h_banks = [psum.tile([P, S], F32, name=f"h{t}") for t in range(PACK)]
        h_last = psum.tile([P, CHUNK], F32, name="h_last")
        z_codes = keep.tile([P, S], U32, name="z_codes", align_bytes=64)
        z_plane = keep.tile([P, S], U8, name="z_plane", align_bytes=64)
        for cols in (slice(0, S - 2 * CHUNK), slice(S - 2 * CHUNK, S - CHUNK), slice(S - CHUNK, S)):
            fetch(PACK - 1, cols)
            larger_of(PACK - 1, cols, larger_d)
            put_z(every, PACK - 1, cols, larger_d)
            nc.vector.quantize_mx(
                out=z_codes[:, cols].bitcast(FP8X4), scales=z_plane[:, cols],
                in_=z_bf[:, cols.start * PACK : cols.stop * PACK],
            )
            bank = h_banks[0][:, cols] if cols.stop < S else h_last[:]
            product(bank, q3[0], 0, z_codes[:, cols], z_plane[:, cols], True, True)
        for t in range(1, PACK):
            product(h_banks[t][:], q3[t // 2], t % 2 * P, z_codes[:], z_plane[:], True, True)

        early, late = slice(0, S - CHUNK), slice(S - CHUNK, S)
        pulled = keep.tile([P, PACK, S], F32, name="pulled")
        for t in range(PACK):
            positive = keep.tile([P, WIDE], F32, name=f"positive{t}")
            if t == 0:
                nc.scalar.activation(positive[:, early], h_banks[0][:, early], RELU)
                nc.scalar.activation(positive[:, late], h_last[:], RELU)
            else:
                nc.vector.tensor_scalar_max(positive[:, 0:S], h_banks[t][:], 0.0)
            nc.scalar.activation(pulled[:, t, :], positive[:].indirect(n4_t[:]), COPY)
        for t in range(PACK):
            nw = keep.tile([P, S], F32, name=f"nw{t}")
            if t == 0:
                nc.vector.tensor_tensor(nw[:, early], h_banks[0][:, early], pulled[:, 0, early], ALU.subtract)
                nc.vector.tensor_tensor(nw[:, late], h_last[:], pulled[:, 0, late], ALU.subtract)
            else:
                nc.vector.tensor_tensor(nw[:], h_banks[t][:], pulled[:, t, :], ALU.subtract)
            nc.scalar.activation(pages[t][:].indirect(n3_t[:]), nw[:], COPY)
            nc.sync.dma_start(out[t * P : (t + 1) * P, :], pages[t][:])
